import numpy as np
import ml_dtypes


def mxq(x, axis, fmt="e4m3"):
    dtype, down = {"e4m3": (ml_dtypes.float8_e4m3fn, 7), "e5m2": (ml_dtypes.float8_e5m2, 14)}[fmt]
    v = np.moveaxis(np.asarray(x, np.float32).astype(ml_dtypes.bfloat16).astype(np.float64), axis, -1)
    blocks = v.reshape(v.shape[:-1] + (-1, 32))
    amax = np.abs(blocks).max(-1, keepdims=True)
    byte = np.maximum(np.where(amax > 0, np.frexp(amax)[1] - 1 + 127, 0) - down, 1)
    scale = np.exp2(byte - 127.0)
    codes = (blocks / scale).astype(np.float32).astype(dtype).astype(np.float64)
    return np.moveaxis((codes * scale).reshape(v.shape), -1, axis)


WIDE = False


def mx_kscale(k):
    if not WIDE:
        return np.ones(k)
    levels = np.array([30, -30])
    if k % 512:
        return np.exp2(np.random.permutation(np.resize(levels, k // 32))).repeat(32)
    a = np.empty((k // 512, 16))
    for p in range(k // 512):
        a[p, :8] = np.random.permutation(np.resize(levels, 8))
        for g in range(8):
            far = levels[np.abs(levels - a[p, g]) >= 10]
            a[p, g + 8] = far[np.random.randint(len(far))]
    return np.exp2(a.ravel()).repeat(32)


BF16 = ml_dtypes.bfloat16


def bf(x):
    return np.asarray(x, np.float32).astype(BF16)


def f64(x):
    return np.asarray(x).astype(np.float64)


M, N, E, J = 1024, 2048, 1024, 1536


def setup_inputs():
    s = mx_kscale(E)
    t = mx_kscale(J)
    queries = np.random.standard_normal((M, E)) * s
    corpus = np.random.standard_normal((N, E)) / np.sqrt(E) / s
    relevance = np.random.standard_normal((J, M)) ** 3 / 4 * t[:, None]
    sim = np.random.standard_normal((J, N)) / np.sqrt(J) / t[:, None]
    return {"queries": bf(queries),
            "corpus": bf(corpus),
            "relevance": bf(relevance),
            "sim": bf(sim),
            "gain": bf(1 + 0.1 * np.random.standard_normal(M)),
            "prior": bf(0.3 * np.random.standard_normal(N))}


def reference(queries, corpus, relevance, sim, gain, prior):
    qq = mxq(f64(queries), 1, "e4m3")
    cq = mxq(f64(corpus), 1, "e4m3")
    rq = mxq(f64(relevance), 0, "e5m2")
    sq = mxq(f64(sim), 0, "e4m3")
    score = (qq @ cq.T) + (rq.T @ sq)
    return score * f64(gain)[:, None] + f64(prior)[None, :]

@@ -1,0 +1,374 @@
+from contextlib import ExitStack
+
+import concourse.mybir as mybir
+from concourse.masks import make_identity
+
+F32 = mybir.dt.float32
+BF16 = mybir.dt.bfloat16
+U32 = mybir.dt.uint32
+U8 = mybir.dt.uint8
+E4M3X4 = mybir.dt.float8_e4m3fn_x4
+E5M2X4 = mybir.dt.float8_e5m2_x4
+MULT = mybir.AluOpType.mult
+ADD = mybir.AluOpType.add
+
+M, N, E, J = 1024, 2048, 1024, 1536
+FLOPS = 2 * M * N * (E + J)
+
+P = 128
+K_PASS = 512
+E_PASSES = E // K_PASS
+J_PASSES = J // K_PASS
+NB = 512
+M_TILES = M // P
+N_BLOCKS = N // NB
+WORDS = E // 2
+
+
+def tile_rocchio_feedback_rescore_s2_kernel(tc, queries, corpus, relevance, sim, gain, prior, out):
+    nc = tc.nc
+    with ExitStack() as ctx:
+        keep = ctx.enter_context(tc.tile_pool(name="keep", bufs=1))
+        raw = ctx.enter_context(tc.tile_pool(name="raw", bufs=1))
+        stage = ctx.enter_context(tc.tile_pool(name="stage", bufs=3))
+        psum = ctx.enter_context(tc.psum_pool(name="psum", bufs=1))
+        ctx.enter_context(tc.manual_schedule())
+
+        ident = keep.tile([P, P], F32, name="ident")
+        ident_bf = keep.tile([P, P], BF16, name="ident_bf")
+        rows = keep.tile([P, P], BF16, name="rows")
+        cols = keep.tile([P, 24], BF16, name="cols")
+        gain_col = keep.tile([P, M_TILES], F32, name="gain_col")
+        prior_bc = keep.tile([P, N], BF16, name="prior_bc")
+
+        q_codes = keep.tile([P, M_TILES, E_PASSES, P], U32, name="q_codes", align_bytes=64)
+        q_scales = keep.tile([P, M_TILES, E_PASSES, P], U8, name="q_scales", align_bytes=64)
+        r_codes = keep.tile([P, J_PASSES, M], U32, name="r_codes", align_bytes=64)
+        r_scales = keep.tile([P, J_PASSES, M], U8, name="r_scales", align_bytes=64)
+        q_raw = raw.tile([P, M_TILES, E], BF16, name="q_raw", align_bytes=64)
+        r_raw = raw.tile([P, J_PASSES, 4, M], BF16, name="r_raw", align_bytes=64)
+        c_raw, s_raw, c_codes, c_scales, s_codes, s_scales = {}, {}, {}, {}, {}, {}
+
+        q_view = queries.rearrange("(t p) e -> p t e", p=P)
+        c_view = corpus.rearrange("(t p) e -> p t e", p=P)
+        r_view = relevance.rearrange("(c p j) m -> c p j m", p=P, j=4)
+        s_view = sim.rearrange("(c p j) n -> c p j n", p=P, j=4)
+
+        def load_q(t0, t1):
+            nc.sync.dma_start(out=q_raw[:, t0:t1, :], in_=q_view[:, t0:t1, :])
+
+        def load_r(c):
+            nc.sync.dma_start(out=r_raw[:, c, :, :], in_=r_view[c])
+
+        def load_c(n):
+            c_raw[n] = raw.tile([P, 4, E], BF16, name="c_raw_t", bufs=2, align_bytes=64)
+            for h in range(2):
+                nc.sync.dma_start(out=c_raw[n][:, 2 * h : 2 * h + 2, :], in_=c_view[:, 4 * n + 2 * h : 4 * n + 2 * h + 2, :])
+
+        def load_s(c, n):
+            s_raw[c, n] = raw.tile([P, 4, NB], BF16, name="s_raw_t", bufs=8, align_bytes=64)
+            nc.sync.dma_start(out=s_raw[c, n][:], in_=s_view[c, :, :, n * NB : (n + 1) * NB])
+
+        def bank_tile(b, shape=(P, NB), dtype=F32):
+            return psum.tile(list(shape), dtype, name="bank_t", tag=f"bank{b}")
+
+        def copy_words(engine, dst, src):
+            if engine == "S":
+                nc.scalar.copy(out=dst, in_=src)
+            else:
+                nc.vector.tensor_copy(out=dst, in_=src)
+
+        def turn(words, bank):
+            for g in range(E_PASSES):
+                for u in range(2):
+                    s = 2 * g + u
+                    nc.tensor.transpose(
+                        bank[:, s * P : (s + 1) * P], words[:, 256 * g + u : 256 * (g + 1) : 2], ident[:]
+                    )
+
+        c_sort = {}
+
+        def sort_c(n, t):
+            if t == 0:
+                c_sort[n] = raw.tile([P, 4, WORDS], F32, name="c_sort_t", bufs=1, align_bytes=64)
+            nc.vector.tensor_copy(
+                out=c_sort[n][:, t, :].rearrange("p (g u w) -> p g u w", g=2, u=2),
+                in_=c_raw[n][:, t, :].bitcast(F32).rearrange("p (g w u) -> p g u w", g=2, u=2),
+            )
+
+        q_bank, q_grp = {}, {}
+
+        def turn_q(m, b):
+            q_bank[m] = bank_tile(b)
+            turn(q_raw[:, m, :].bitcast(F32), q_bank[m])
+
+        def copy_q(m, engine):
+            q_grp[m] = stage.tile([P, E_PASSES, P, 4], BF16, name="q_grp_t", align_bytes=64)
+            copy_words(
+                engine,
+                q_grp[m][:].rearrange("p g r j -> p (g r j)").bitcast(F32).rearrange("p (g r u) -> p g r u", g=2, u=2),
+                q_bank[m][:].rearrange("p (g u r) -> p g r u", g=2, u=2),
+            )
+
+        def quant_q(m):
+            nc.vector.quantize_mx(
+                out=q_codes[:, m, :, :].rearrange("p g r -> p (g r)").bitcast(E4M3X4),
+                scales=q_scales[:, m, :, :].rearrange("p g r -> p (g r)"),
+                in_=q_grp[m][:].rearrange("p g r j -> p (g r j)"),
+            )
+
+        c_bank, c_grp = {}, {}
+
+        def turn_c(n, t, b):
+            c_bank[n, t] = bank_tile(b)
+            if n < 2:
+                turn(c_raw[n][:, t, :].bitcast(F32), c_bank[n, t])
+            else:
+                for s in range(4):
+                    nc.tensor.transpose(
+                        c_bank[n, t][:, s * P : (s + 1) * P], c_sort[n][:, t, s * P : (s + 1) * P], ident[:]
+                    )
+
+        def copy_c(n, t, engine):
+            if t == 0:
+                c_grp[n] = stage.tile([P, E_PASSES, NB, 4], BF16, name="c_grp_t", bufs=2, align_bytes=64)
+            words = c_grp[n][:].rearrange("p g r j -> p (g r j)").bitcast(F32)
+            copy_words(
+                engine,
+                words.rearrange("p (g r u) -> p g r u", g=2, u=2)[:, :, t * P : (t + 1) * P, :],
+                c_bank[n, t][:].rearrange("p (g u r) -> p g r u", g=2, u=2),
+            )
+
+        def quant_c(n, g):
+            if g == 0:
+                c_codes[n] = stage.tile([P, E_PASSES, NB], U32, name="c_codes_t", bufs=2, align_bytes=64)
+                c_scales[n] = stage.tile([P, E_PASSES, NB], U8, name="c_scales_t", bufs=2, align_bytes=64)
+            nc.vector.quantize_mx(
+                out=c_codes[n][:, g, :].bitcast(E4M3X4),
+                scales=c_scales[n][:, g, :],
+                in_=c_grp[n][:, g, :, :].rearrange("p r j -> p (r j)"),
+            )
+
+        r_grp, s_grp = {}, {}
+
+        def copy_r(c, h, engine):
+            r_grp[c, h] = stage.tile([P, NB, 4], BF16, name="k_grp_t", bufs=6, align_bytes=64)
+            copy_words(engine, r_grp[c, h][:], r_raw[:, c, :, h * NB : (h + 1) * NB].rearrange("p j w -> p w j"))
+
+        def quant_r(c, h):
+            nc.vector.quantize_mx(
+                out=r_codes[:, c, h * NB : (h + 1) * NB].bitcast(E5M2X4),
+                scales=r_scales[:, c, h * NB : (h + 1) * NB],
+                in_=r_grp[c, h][:].rearrange("p w j -> p (w j)"),
+            )
+
+        def copy_s(c, n, engines):
+            s_grp[c, n] = stage.tile([P, NB, 4], BF16, name="k_grp_t", bufs=6, align_bytes=64)
+            w = NB // len(engines)
+            for i, engine in enumerate(engines):
+                cs = slice(i * w, (i + 1) * w)
+                copy_words(engine, s_grp[c, n][:, cs, :], s_raw[c, n][:, :, cs].rearrange("p j w -> p w j"))
+
+        def quant_s(c, n):
+            s_codes[c, n] = stage.tile([P, NB], U32, name="s_codes_t", bufs=7, align_bytes=64)
+            s_scales[c, n] = stage.tile([P, NB], U8, name="s_scales_t", bufs=7, align_bytes=64)
+            nc.vector.quantize_mx(
+                out=s_codes[c, n][:].bitcast(E4M3X4),
+                scales=s_scales[c, n][:],
+                in_=s_grp[c, n][:].rearrange("p w j -> p (w j)"),
+            )
+
+        acc = {}
+
+        def pass_qc(n, m, g, b):
+            if g == 0:
+                acc[n, m] = bank_tile(b)
+            nc.tensor.matmul_mx(
+                out=acc[n, m][:],
+                lhsT=q_codes[:, m, g, :].bitcast(E4M3X4),
+                lhsT_scale=q_scales[:, m, g, :],
+                rhs=c_codes[n][:, g, :].bitcast(E4M3X4),
+                rhs_scale=c_scales[n][:, g, :],
+                start=(g == 0),
+                stop=False,
+            )
+
+        def pass_rs(n, m, c):
+            nc.tensor.matmul_mx(
+                out=acc[n, m][:],
+                lhsT=r_codes[:, c, m * P : (m + 1) * P].bitcast(E5M2X4),
+                lhsT_scale=r_scales[:, c, m * P : (m + 1) * P],
+                rhs=s_codes[c, n][:].bitcast(E4M3X4),
+                rhs_scale=s_scales[c, n][:],
+                start=False,
+                stop=(c == J_PASSES - 1),
+            )
+
+        def finish(n, m, pieces=1):
+            res = stage.tile([P, NB], F32, name="res_t", bufs=8)
+            w = NB // pieces
+            for i in range(pieces):
+                cs = slice(i * w, (i + 1) * w)
+                oc = slice(n * NB + i * w, n * NB + (i + 1) * w)
+                nc.vector.scalar_tensor_tensor(
+                    out=res[:, cs],
+                    in0=acc[n, m][:, cs],
+                    scalar=gain_col[:, m : m + 1],
+                    in1=prior_bc[:, oc],
+                    op0=MULT,
+                    op1=ADD,
+                )
+                nc.sync.dma_start(out=out[m * P : (m + 1) * P, oc], in_=res[:, cs])
+
+        V, S = "V", "S"
+        halves = (range(0, 4), range(4, 8))
+
+        nc.vector.memset(rows[:], 0.0)
+        nc.scalar.dma_start(out=rows[0:16, :], in_=prior.rearrange("(a b) -> a b", b=P))
+        nc.scalar.dma_start(out=rows[16:24, :], in_=gain.rearrange("(a b) -> a b", b=P))
+        load_q(0, 1)
+        load_q(1, 2)
+        load_r(0)
+        load_q(2, 4)
+        load_q(4, 6)
+        load_q(6, 8)
+        load_c(0)
+        load_s(0, 0)
+        load_r(1)
+        load_s(1, 0)
+        load_r(2)
+        load_s(2, 0)
+        load_c(1)
+        for c in range(3):
+            load_s(c, 1)
+
+        make_identity(nc, ident[:])
+        nc.vector.tensor_copy(out=ident_bf[:], in_=ident[:])
+
+        turn_q(0, 0)
+        copy_q(0, S)
+        turn_q(1, 1)
+        copy_q(1, S)
+        rows_t = bank_tile(2, (P, P), BF16)
+        nc.tensor.transpose(rows_t[:], rows[:], ident_bf[:])
+        nc.vector.tensor_copy(out=cols[:], in_=rows_t[:, 0:24])
+        nc.vector.tensor_copy(out=gain_col[:], in_=rows_t[:, 16:24])
+        spread = {}
+        for h in range(2):
+            spread[h] = bank_tile(3 + h, (P, M), BF16)
+            for i in range(8):
+                nc.tensor.transpose(
+                    spread[h][:, i * P : (i + 1) * P], cols[:, 8 * h + i : 8 * h + i + 1].to_broadcast([P, P]), ident_bf[:]
+                )
+        quant_q(0)
+        quant_q(1)
+        for h in range(2):
+            copy_words((V, S)[h], prior_bc[:, h * M : (h + 1) * M], spread[h][:])
+        copy_r(0, 0, V)
+        copy_r(0, 1, S)
+        for m in range(2, 8):
+            turn_q(m, (5, 6, 7, 0, 1, 2)[m - 2])
+            copy_q(m, V if m < 4 else S)
+            if m == 4:
+                quant_r(0, 0)
+            if m > 3:
+                quant_q(m - 1) if m != 4 else quant_q(2)
+        quant_q(3)
+        quant_r(0, 1)
+        for t in range(4):
+            turn_c(0, t, 3 + t)
+            copy_c(0, t, (V, S)[t % 2])
+        quant_q(7)
+        quant_c(0, 0)
+        quant_c(0, 1)
+        for g in range(2):
+            for m in range(8):
+                pass_qc(0, m, g, m)
+        copy_s(0, 0, S)
+        copy_r(1, 0, V)
+        copy_r(1, 1, V)
+        quant_r(1, 0)
+        quant_s(0, 0)
+        quant_r(1, 1)
+        copy_s(1, 0, S)
+        for m in range(8):
+            pass_rs(0, m, 0)
+        copy_r(2, 0, V)
+        copy_r(2, 1, S)
+        quant_s(1, 0)
+        copy_s(2, 0, V + S)
+        quant_r(2, 0)
+        for m in range(8):
+            pass_rs(0, m, 1)
+        quant_s(2, 0)
+        quant_r(2, 1)
+        load_c(2)
+        for c in range(3):
+            load_s(c, 2)
+        for m in range(0, 4):
+            pass_rs(0, m, 2)
+        for m in range(0, 4):
+            finish(0, m)
+        copy_s(0, 1, S)
+        for h in range(2):
+            for t in (2 * h, 2 * h + 1):
+                turn_c(1, t, t)
+                copy_c(1, t, S)
+            for m in (4 + 2 * h, 5 + 2 * h):
+                pass_rs(0, m, 2)
+        finish(0, 4)
+        quant_c(1, 0)
+        quant_c(1, 1)
+        finish(0, 5)
+        finish(0, 6)
+        finish(0, 7)
+        quant_s(0, 1)
+        copy_s(1, 1, V + S)
+        copy_s(2, 1, V + S)
+        quant_s(1, 1)
+
+        for n in range(1, N_BLOCKS):
+            more = n + 1 < N_BLOCKS
+            t_at = 4 if n == 1 else 3
+            if n == 1:
+                load_c(3)
+                for c in range(3):
+                    load_s(c, 3)
+                for ms in (range(0, 4), range(4, 8)):
+                    for g in range(2):
+                        for m in ms:
+                            pass_qc(n, m, g, m)
+                quant_s(2, 1)
+                for t in range(4):
+                    sort_c(2, t)
+                for c in range(2):
+                    for m in range(4):
+                        pass_rs(n, m, c)
+            for m in range(M_TILES):
+                if n > 1:
+                    for g in range(2):
+                        pass_qc(n, m, g, m)
+                for c in range(2 if n == 1 and m < 4 else 0, 3):
+                    pass_rs(n, m, c)
+                if more:
+                    if m == 0:
+                        copy_s(0, n + 1, S)
+                    if m == 2:
+                        copy_s(1, n + 1, S)
+                    if m == 3:
+                        quant_s(0, n + 1)
+                    if m < 4 and n == 2:
+                        sort_c(n + 1, m)
+                    if m == t_at:
+                        for t in range(4):
+                            turn_c(n + 1, t, t if t < t_at else 7)
+                            copy_c(n + 1, t, S)
+                finish(n, m, 2 if m == 7 and not more else 1)
+                if more:
+                    if m == t_at + 1:
+                        copy_s(2, n + 1, V + S)
+                        quant_c(n + 1, 0)
+                        quant_c(n + 1, 1)
+                    if m == t_at + 2:
+                        quant_s(1, n + 1)
+                        quant_s(2, n + 1)

@@ -151,9 +151,16 @@ def tile_rocchio_feedback_rescore_s2_kernel(tc, queries, corpus, relevance, sim,
 
         r_grp, s_grp = {}, {}
 
+        def interleave(engine, dst, src):
+            copy_words(
+                engine,
+                dst.rearrange("p (c i) j -> p c j i", i=4),
+                src.rearrange("p j (c i) -> p c j i", i=4),
+            )
+
         def copy_r(c, h, engine):
             r_grp[c, h] = stage.tile([P, NB, 4], BF16, name="k_grp_t", bufs=6, align_bytes=64)
-            copy_words(engine, r_grp[c, h][:], r_raw[:, c, :, h * NB : (h + 1) * NB].rearrange("p j w -> p w j"))
+            interleave(engine, r_grp[c, h][:], r_raw[:, c, :, h * NB : (h + 1) * NB])
 
         def quant_r(c, h):
             nc.vector.quantize_mx(
@@ -167,7 +174,7 @@ def tile_rocchio_feedback_rescore_s2_kernel(tc, queries, corpus, relevance, sim,
             w = NB // len(engines)
             for i, engine in enumerate(engines):
                 cs = slice(i * w, (i + 1) * w)
-                copy_words(engine, s_grp[c, n][:, cs, :], s_raw[c, n][:, :, cs].rearrange("p j w -> p w j"))
+                interleave(engine, s_grp[c, n][:, cs, :], s_raw[c, n][:, :, cs])
 
         def quant_s(c, n):
             s_codes[c, n] = stage.tile([P, NB], U32, name="s_codes_t", bufs=7, align_bytes=64)
@@ -224,10 +231,10 @@ def tile_rocchio_feedback_rescore_s2_kernel(tc, queries, corpus, relevance, sim,
         halves = (range(0, 4), range(4, 8))
 
         nc.vector.memset(rows[:], 0.0)
-        nc.scalar.dma_start(out=rows[0:16, :], in_=prior.rearrange("(a b) -> a b", b=P))
-        nc.scalar.dma_start(out=rows[16:24, :], in_=gain.rearrange("(a b) -> a b", b=P))
         load_q(0, 1)
         load_q(1, 2)
+        nc.sync.dma_start(out=rows[0:16, :], in_=prior.rearrange("(a b) -> a b", b=P))
+        nc.sync.dma_start(out=rows[16:24, :], in_=gain.rearrange("(a b) -> a b", b=P))
         load_r(0)
         load_q(2, 4)
         load_q(4, 6)
@@ -249,23 +256,14 @@ def tile_rocchio_feedback_rescore_s2_kernel(tc, queries, corpus, relevance, sim,
         copy_q(0, S)
         turn_q(1, 1)
         copy_q(1, S)
+        quant_q(0)
+        quant_q(1)
+        copy_r(0, 0, V)
+        copy_r(0, 1, S)
         rows_t = bank_tile(2, (P, P), BF16)
         nc.tensor.transpose(rows_t[:], rows[:], ident_bf[:])
         nc.vector.tensor_copy(out=cols[:], in_=rows_t[:, 0:24])
         nc.vector.tensor_copy(out=gain_col[:], in_=rows_t[:, 16:24])
-        spread = {}
-        for h in range(2):
-            spread[h] = bank_tile(3 + h, (P, M), BF16)
-            for i in range(8):
-                nc.tensor.transpose(
-                    spread[h][:, i * P : (i + 1) * P], cols[:, 8 * h + i : 8 * h + i + 1].to_broadcast([P, P]), ident_bf[:]
-                )
-        quant_q(0)
-        quant_q(1)
-        for h in range(2):
-            copy_words((V, S)[h], prior_bc[:, h * M : (h + 1) * M], spread[h][:])
-        copy_r(0, 0, V)
-        copy_r(0, 1, S)
         for m in range(2, 8):
             turn_q(m, (5, 6, 7, 0, 1, 2)[m - 2])
             copy_q(m, V if m < 4 else S)
@@ -278,6 +276,14 @@ def tile_rocchio_feedback_rescore_s2_kernel(tc, queries, corpus, relevance, sim,
         for t in range(4):
             turn_c(0, t, 3 + t)
             copy_c(0, t, (V, S)[t % 2])
+        spread = {}
+        for h in range(2):
+            spread[h] = bank_tile((7, 2)[h], (P, M), BF16)
+            for i in range(8):
+                nc.tensor.transpose(
+                    spread[h][:, i * P : (i + 1) * P], cols[:, 8 * h + i : 8 * h + i + 1].to_broadcast([P, P]), ident_bf[:]
+                )
+            copy_words(S, prior_bc[:, h * M : (h + 1) * M], spread[h][:])
         quant_q(7)
         quant_c(0, 0)
         quant_c(0, 1)

@@ -37,16 +37,15 @@ def tile_rocchio_feedback_rescore_s2_kernel(tc, queries, corpus, relevance, sim,
         ident = keep.tile([P, P], F32, name="ident")
         ident_bf = keep.tile([P, P], BF16, name="ident_bf")
         rows = keep.tile([P, P], BF16, name="rows")
-        cols = keep.tile([P, 24], BF16, name="cols")
         gain_col = keep.tile([P, M_TILES], F32, name="gain_col")
-        prior_bc = keep.tile([P, N], BF16, name="prior_bc")
+        prior_bc = keep.tile([P, N_BLOCKS, NB], BF16, name="prior_bc")
 
-        q_codes = keep.tile([P, M_TILES, E_PASSES, P], U32, name="q_codes", align_bytes=64)
-        q_scales = keep.tile([P, M_TILES, E_PASSES, P], U8, name="q_scales", align_bytes=64)
-        r_codes = keep.tile([P, J_PASSES, M], U32, name="r_codes", align_bytes=64)
-        r_scales = keep.tile([P, J_PASSES, M], U8, name="r_scales", align_bytes=64)
-        q_raw = raw.tile([P, M_TILES, E], BF16, name="q_raw", align_bytes=64)
-        r_raw = raw.tile([P, J_PASSES, 4, M], BF16, name="r_raw", align_bytes=64)
+        q_codes = keep.tile([P, M_TILES, E_PASSES, P], U32, name="q_codes", align_bytes=256)
+        q_scales = keep.tile([P, M_TILES, E_PASSES, P], U8, name="q_scales", align_bytes=256)
+        r_codes = keep.tile([P, J_PASSES, M], U32, name="r_codes", align_bytes=256)
+        r_scales = keep.tile([P, J_PASSES, M], U8, name="r_scales", align_bytes=256)
+        q_raw = raw.tile([P, M_TILES, E], BF16, name="q_raw", align_bytes=256)
+        r_raw = raw.tile([P, J_PASSES, 4, M], BF16, name="r_raw", align_bytes=256)
         c_raw, s_raw, c_codes, c_scales, s_codes, s_scales = {}, {}, {}, {}, {}, {}
 
         q_view = queries.rearrange("(t p) e -> p t e", p=P)
@@ -61,12 +60,16 @@ def tile_rocchio_feedback_rescore_s2_kernel(tc, queries, corpus, relevance, sim,
             nc.sync.dma_start(out=r_raw[:, c, :, :], in_=r_view[c])
 
         def load_c(n):
-            c_raw[n] = raw.tile([P, 4, E], BF16, name="c_raw_t", bufs=2, align_bytes=64)
-            for h in range(2):
-                nc.sync.dma_start(out=c_raw[n][:, 2 * h : 2 * h + 2, :], in_=c_view[:, 4 * n + 2 * h : 4 * n + 2 * h + 2, :])
+            c_raw[n] = raw.tile([P, 4, E], BF16, name="c_raw_t", bufs=2, align_bytes=256)
+            step = 1 if n == 0 else 2
+            for t in range(0, 4, step):
+                nc.sync.dma_start(out=c_raw[n][:, t : t + step, :], in_=c_view[:, 4 * n + t : 4 * n + t + step, :])
+
+        def load_prior(n):
+            nc.sync.dma_start(out=prior_bc[:, n, :], in_=prior[n * NB : (n + 1) * NB].partition_broadcast(P))
 
         def load_s(c, n):
-            s_raw[c, n] = raw.tile([P, 4, NB], BF16, name="s_raw_t", bufs=8, align_bytes=64)
+            s_raw[c, n] = raw.tile([P, 4, NB], BF16, name="s_raw_t", bufs=8, align_bytes=256)
             nc.sync.dma_start(out=s_raw[c, n][:], in_=s_view[c, :, :, n * NB : (n + 1) * NB])
 
         def bank_tile(b, shape=(P, NB), dtype=F32):
@@ -90,7 +93,7 @@ def tile_rocchio_feedback_rescore_s2_kernel(tc, queries, corpus, relevance, sim,
 
         def sort_c(n, t):
             if t == 0:
-                c_sort[n] = raw.tile([P, 4, WORDS], F32, name="c_sort_t", bufs=1, align_bytes=64)
+                c_sort[n] = raw.tile([P, 4, WORDS], F32, name="c_sort_t", bufs=1, align_bytes=256)
             nc.vector.tensor_copy(
                 out=c_sort[n][:, t, :].rearrange("p (g u w) -> p g u w", g=2, u=2),
                 in_=c_raw[n][:, t, :].bitcast(F32).rearrange("p (g w u) -> p g u w", g=2, u=2),
@@ -103,7 +106,7 @@ def tile_rocchio_feedback_rescore_s2_kernel(tc, queries, corpus, relevance, sim,
             turn(q_raw[:, m, :].bitcast(F32), q_bank[m])
 
         def copy_q(m, engine):
-            q_grp[m] = stage.tile([P, E_PASSES, P, 4], BF16, name="q_grp_t", align_bytes=64)
+            q_grp[m] = stage.tile([P, E_PASSES, P, 4], BF16, name="q_grp_t", align_bytes=256)
             copy_words(
                 engine,
                 q_grp[m][:].rearrange("p g r j -> p (g r j)").bitcast(F32).rearrange("p (g r u) -> p g r u", g=2, u=2),
@@ -131,7 +134,7 @@ def tile_rocchio_feedback_rescore_s2_kernel(tc, queries, corpus, relevance, sim,
 
         def copy_c(n, t, engine):
             if t == 0:
-                c_grp[n] = stage.tile([P, E_PASSES, NB, 4], BF16, name="c_grp_t", bufs=2, align_bytes=64)
+                c_grp[n] = stage.tile([P, E_PASSES, NB, 4], BF16, name="c_grp_t", bufs=2, align_bytes=256)
             words = c_grp[n][:].rearrange("p g r j -> p (g r j)").bitcast(F32)
             copy_words(
                 engine,
@@ -139,14 +142,15 @@ def tile_rocchio_feedback_rescore_s2_kernel(tc, queries, corpus, relevance, sim,
                 c_bank[n, t][:].rearrange("p (g u r) -> p g r u", g=2, u=2),
             )
 
-        def quant_c(n, g):
-            if g == 0:
-                c_codes[n] = stage.tile([P, E_PASSES, NB], U32, name="c_codes_t", bufs=2, align_bytes=64)
-                c_scales[n] = stage.tile([P, E_PASSES, NB], U8, name="c_scales_t", bufs=2, align_bytes=64)
+        def quant_c(n, g, h):
+            if g == 0 and h == 0:
+                c_codes[n] = stage.tile([P, E_PASSES, NB], U32, name="c_codes_t", bufs=2, align_bytes=256)
+                c_scales[n] = stage.tile([P, E_PASSES, NB], U8, name="c_scales_t", bufs=2, align_bytes=256)
+            cs = slice(h * 256, (h + 1) * 256)
             nc.vector.quantize_mx(
-                out=c_codes[n][:, g, :].bitcast(E4M3X4),
-                scales=c_scales[n][:, g, :],
-                in_=c_grp[n][:, g, :, :].rearrange("p r j -> p (r j)"),
+                out=c_codes[n][:, g, cs].bitcast(E4M3X4),
+                scales=c_scales[n][:, g, cs],
+                in_=c_grp[n][:, g, cs, :].rearrange("p r j -> p (r j)"),
             )
 
         r_grp, s_grp = {}, {}
@@ -159,7 +163,7 @@ def tile_rocchio_feedback_rescore_s2_kernel(tc, queries, corpus, relevance, sim,
             )
 
         def copy_r(c, h, engine):
-            r_grp[c, h] = stage.tile([P, NB, 4], BF16, name="k_grp_t", bufs=6, align_bytes=64)
+            r_grp[c, h] = stage.tile([P, NB, 4], BF16, name="k_grp_t", bufs=6, align_bytes=256)
             interleave(engine, r_grp[c, h][:], r_raw[:, c, :, h * NB : (h + 1) * NB])
 
         def quant_r(c, h):
@@ -170,15 +174,15 @@ def tile_rocchio_feedback_rescore_s2_kernel(tc, queries, corpus, relevance, sim,
             )
 
         def copy_s(c, n, engines):
-            s_grp[c, n] = stage.tile([P, NB, 4], BF16, name="k_grp_t", bufs=6, align_bytes=64)
+            s_grp[c, n] = stage.tile([P, NB, 4], BF16, name="k_grp_t", bufs=6, align_bytes=256)
             w = NB // len(engines)
             for i, engine in enumerate(engines):
                 cs = slice(i * w, (i + 1) * w)
                 interleave(engine, s_grp[c, n][:, cs, :], s_raw[c, n][:, :, cs])
 
         def quant_s(c, n):
-            s_codes[c, n] = stage.tile([P, NB], U32, name="s_codes_t", bufs=7, align_bytes=64)
-            s_scales[c, n] = stage.tile([P, NB], U8, name="s_scales_t", bufs=7, align_bytes=64)
+            s_codes[c, n] = stage.tile([P, NB], U32, name="s_codes_t", bufs=7, align_bytes=256)
+            s_scales[c, n] = stage.tile([P, NB], U8, name="s_scales_t", bufs=7, align_bytes=256)
             nc.vector.quantize_mx(
                 out=s_codes[c, n][:].bitcast(E4M3X4),
                 scales=s_scales[c, n][:],
@@ -221,11 +225,20 @@ def tile_rocchio_feedback_rescore_s2_kernel(tc, queries, corpus, relevance, sim,
                     out=res[:, cs],
                     in0=acc[n, m][:, cs],
                     scalar=gain_col[:, m : m + 1],
-                    in1=prior_bc[:, oc],
+                    in1=prior_bc[:, n, cs],
                     op0=MULT,
                     op1=ADD,
                 )
                 nc.sync.dma_start(out=out[m * P : (m + 1) * P, oc], in_=res[:, cs])
+
+        def finish_sg(n, m):
+            part = stage.tile([P, NB], F32, name="part_t", bufs=2)
+            res = stage.tile([P, NB], F32, name="res_t", bufs=8)
+            nc.scalar.activation(
+                out=part[:], in_=acc[n, m][:], func=mybir.ActivationFunctionType.Copy, scale=gain_col[:, m : m + 1]
+            )
+            nc.gpsimd.tensor_tensor(out=res[:], in0=part[:], in1=prior_bc[:, n, :], op=ADD)
+            nc.sync.dma_start(out=out[m * P : (m + 1) * P, n * NB : (n + 1) * NB], in_=res[:])
 
         V, S = "V", "S"
         halves = (range(0, 4), range(4, 8))
@@ -233,69 +246,67 @@ def tile_rocchio_feedback_rescore_s2_kernel(tc, queries, corpus, relevance, sim,
         nc.vector.memset(rows[:], 0.0)
         load_q(0, 1)
         load_q(1, 2)
-        nc.sync.dma_start(out=rows[0:16, :], in_=prior.rearrange("(a b) -> a b", b=P))
-        nc.sync.dma_start(out=rows[16:24, :], in_=gain.rearrange("(a b) -> a b", b=P))
-        load_r(0)
         load_q(2, 4)
+        nc.sync.dma_start(out=rows[0:8, :], in_=gain.rearrange("(a b) -> a b", b=P))
+        load_r(0)
         load_q(4, 6)
         load_q(6, 8)
         load_c(0)
-        load_s(0, 0)
         load_r(1)
+        load_s(0, 0)
         load_s(1, 0)
         load_r(2)
+        load_prior(0)
         load_s(2, 0)
         load_c(1)
         for c in range(3):
             load_s(c, 1)
+        load_prior(1)
 
         make_identity(nc, ident[:])
         nc.vector.tensor_copy(out=ident_bf[:], in_=ident[:])
 
-        turn_q(0, 0)
-        copy_q(0, S)
-        turn_q(1, 1)
-        copy_q(1, S)
+        for m in (0, 1):
+            turn_q(m, m)
+            copy_q(m, S)
         quant_q(0)
         quant_q(1)
         copy_r(0, 0, V)
         copy_r(0, 1, S)
-        rows_t = bank_tile(2, (P, P), BF16)
+        for m in (2, 3):
+            turn_q(m, m)
+            copy_q(m, V)
+        quant_r(0, 0)
+        for m in range(4, 8):
+            turn_q(m, m)
+            copy_q(m, S)
+        rows_t = bank_tile(0, (P, P), BF16)
         nc.tensor.transpose(rows_t[:], rows[:], ident_bf[:])
-        nc.vector.tensor_copy(out=cols[:], in_=rows_t[:, 0:24])
-        nc.vector.tensor_copy(out=gain_col[:], in_=rows_t[:, 16:24])
-        for m in range(2, 8):
-            turn_q(m, (5, 6, 7, 0, 1, 2)[m - 2])
-            copy_q(m, V if m < 4 else S)
-            if m == 4:
-                quant_r(0, 0)
-            if m > 3:
-                quant_q(m - 1) if m != 4 else quant_q(2)
+        quant_q(2)
         quant_q(3)
         quant_r(0, 1)
+        quant_q(4)
+        quant_q(5)
+        quant_q(6)
         for t in range(4):
-            turn_c(0, t, 3 + t)
-            copy_c(0, t, (V, S)[t % 2])
-        spread = {}
-        for h in range(2):
-            spread[h] = bank_tile((7, 2)[h], (P, M), BF16)
-            for i in range(8):
-                nc.tensor.transpose(
-                    spread[h][:, i * P : (i + 1) * P], cols[:, 8 * h + i : 8 * h + i + 1].to_broadcast([P, P]), ident_bf[:]
-                )
-            copy_words(S, prior_bc[:, h * M : (h + 1) * M], spread[h][:])
-        quant_q(7)
-        quant_c(0, 0)
-        quant_c(0, 1)
+            turn_c(0, t, 1 + t)
+            copy_c(0, t, (S, V)[t % 2])
+            if t == 2:
+                quant_q(7)
+                nc.vector.tensor_copy(out=gain_col[:], in_=rows_t[:, 0:8])
+                quant_c(0, 0, 0)
+        quant_c(0, 0, 1)
+        quant_c(0, 1, 0)
+        quant_c(0, 1, 1)
         for g in range(2):
             for m in range(8):
                 pass_qc(0, m, g, m)
-        copy_s(0, 0, S)
-        copy_r(1, 0, V)
+        copy_r(1, 0, S)
         copy_r(1, 1, V)
-        quant_r(1, 0)
-        quant_s(0, 0)
+        copy_s(0, 0, V)
         quant_r(1, 1)
+        quant_s(0, 0)
+        quant_r(1, 0)
         copy_s(1, 0, S)
         for m in range(8):
             pass_rs(0, m, 0)
@@ -311,11 +322,13 @@ def tile_rocchio_feedback_rescore_s2_kernel(tc, queries, corpus, relevance, sim,
         load_c(2)
         for c in range(3):
             load_s(c, 2)
+        load_prior(2)
         for m in range(0, 4):
             pass_rs(0, m, 2)
-        for m in range(0, 4):
-            finish(0, m)
-        copy_s(0, 1, S)
+        finish(0, 0)
+        finish_sg(0, 1)
+        finish(0, 2)
+        finish_sg(0, 3)
         for h in range(2):
             for t in (2 * h, 2 * h + 1):
                 turn_c(1, t, t)
@@ -323,41 +336,54 @@ def tile_rocchio_feedback_rescore_s2_kernel(tc, queries, corpus, relevance, sim,
             for m in (4 + 2 * h, 5 + 2 * h):
                 pass_rs(0, m, 2)
         finish(0, 4)
-        quant_c(1, 0)
-        quant_c(1, 1)
+        for g in range(2):
+            quant_c(1, g, 0)
         finish(0, 5)
+        for g in range(2):
+            quant_c(1, g, 1)
         finish(0, 6)
         finish(0, 7)
-        quant_s(0, 1)
+        copy_s(0, 1, V + S)
         copy_s(1, 1, V + S)
+        quant_s(0, 1)
         copy_s(2, 1, V + S)
         quant_s(1, 1)
 
+        load_c(3)
+        for c in range(3):
+            load_s(c, 3)
+        load_prior(3)
         for n in range(1, N_BLOCKS):
             more = n + 1 < N_BLOCKS
-            t_at = 4 if n == 1 else 3
             if n == 1:
-                load_c(3)
-                for c in range(3):
-                    load_s(c, 3)
-                for ms in (range(0, 4), range(4, 8)):
-                    for g in range(2):
-                        for m in ms:
-                            pass_qc(n, m, g, m)
+                for g in range(2):
+                    for m in range(6):
+                        pass_qc(n, m, g, m)
                 quant_s(2, 1)
                 for t in range(4):
                     sort_c(2, t)
+                copy_s(0, 2, S)
                 for c in range(2):
                     for m in range(4):
                         pass_rs(n, m, c)
+                for h in range(2):
+                    for t in (2 * h, 2 * h + 1):
+                        turn_c(2, t, 6 + t % 2)
+                        copy_c(2, t, S)
+                    for m in (2 * h, 2 * h + 1):
+                        pass_rs(n, m, 2)
+                        finish(n, m)
+                    for g in range(2):
+                        quant_c(2, g, h)
             for m in range(M_TILES):
-                if n > 1:
+                if n > 1 or m > 5:
                     for g in range(2):
                         pass_qc(n, m, g, m)
-                for c in range(2 if n == 1 and m < 4 else 0, 3):
-                    pass_rs(n, m, c)
+                if n > 1 or m > 3:
+                    for c in range(3):
+                        pass_rs(n, m, c)
                 if more:
-                    if m == 0:
+                    if m == 0 and n == 2:
                         copy_s(0, n + 1, S)
                     if m == 2:
                         copy_s(1, n + 1, S)
@@ -365,16 +391,19 @@ def tile_rocchio_feedback_rescore_s2_kernel(tc, queries, corpus, relevance, sim,
                         quant_s(0, n + 1)
                     if m < 4 and n == 2:
                         sort_c(n + 1, m)
-                    if m == t_at:
+                    if m == 3 and n == 2:
                         for t in range(4):
-                            turn_c(n + 1, t, t if t < t_at else 7)
+                            turn_c(n + 1, t, t if t < 3 else 7)
                             copy_c(n + 1, t, S)
-                finish(n, m, 2 if m == 7 and not more else 1)
+                if n > 1 or m > 3:
+                    finish(n, m, 2 if m == 7 and not more else 1)
                 if more:
-                    if m == t_at + 1:
+                    if m == 4:
                         copy_s(2, n + 1, V + S)
-                        quant_c(n + 1, 0)
-                        quant_c(n + 1, 1)
-                    if m == t_at + 2:
+                        if n == 2:
+                            for h in range(2):
+                                for g in range(2):
+                                    quant_c(n + 1, g, h)
+                    if m == 5:
                         quant_s(1, n + 1)
                         quant_s(2, n + 1)

@@ -37,6 +37,7 @@ def tile_rocchio_feedback_rescore_s2_kernel(tc, queries, corpus, relevance, sim,
         ident = keep.tile([P, P], F32, name="ident")
         ident_bf = keep.tile([P, P], BF16, name="ident_bf")
         rows = keep.tile([P, P], BF16, name="rows")
+        cols = keep.tile([P, 24], BF16, name="cols")
         gain_col = keep.tile([P, M_TILES], F32, name="gain_col")
         prior_bc = keep.tile([P, N_BLOCKS, NB], BF16, name="prior_bc")
 
@@ -45,8 +46,7 @@ def tile_rocchio_feedback_rescore_s2_kernel(tc, queries, corpus, relevance, sim,
         r_codes = keep.tile([P, J_PASSES, M], U32, name="r_codes", align_bytes=256)
         r_scales = keep.tile([P, J_PASSES, M], U8, name="r_scales", align_bytes=256)
         q_raw = raw.tile([P, M_TILES, E], BF16, name="q_raw", align_bytes=256)
-        r_raw = raw.tile([P, J_PASSES, 4, M], BF16, name="r_raw", align_bytes=256)
-        c_raw, s_raw, c_codes, c_scales, s_codes, s_scales = {}, {}, {}, {}, {}, {}
+        r_raw, c_raw, s_raw, c_codes, c_scales, s_codes, s_scales = {}, {}, {}, {}, {}, {}, {}
 
         q_view = queries.rearrange("(t p) e -> p t e", p=P)
         c_view = corpus.rearrange("(t p) e -> p t e", p=P)
@@ -57,20 +57,25 @@ def tile_rocchio_feedback_rescore_s2_kernel(tc, queries, corpus, relevance, sim,
             nc.sync.dma_start(out=q_raw[:, t0:t1, :], in_=q_view[:, t0:t1, :])
 
         def load_r(c):
-            nc.sync.dma_start(out=r_raw[:, c, :, :], in_=r_view[c])
+            r_raw[c] = raw.tile([P, 4, M], BF16, name="wide_raw_t", bufs=3, align_bytes=256)
+            nc.sync.dma_start(out=r_raw[c][:], in_=r_view[c])
 
         def load_c(n):
-            c_raw[n] = raw.tile([P, 4, E], BF16, name="c_raw_t", bufs=2, align_bytes=256)
+            c_raw[n] = raw.tile([P, 4, E], BF16, name="c_raw_t", bufs=3, align_bytes=256)
             step = 1 if n == 0 else 2
             for t in range(0, 4, step):
                 nc.sync.dma_start(out=c_raw[n][:, t : t + step, :], in_=c_view[:, 4 * n + t : 4 * n + t + step, :])
 
-        def load_prior(n):
-            nc.sync.dma_start(out=prior_bc[:, n, :], in_=prior[n * NB : (n + 1) * NB].partition_broadcast(P))
-
         def load_s(c, n):
-            s_raw[c, n] = raw.tile([P, 4, NB], BF16, name="s_raw_t", bufs=8, align_bytes=256)
-            nc.sync.dma_start(out=s_raw[c, n][:], in_=s_view[c, :, :, n * NB : (n + 1) * NB])
+            tile_s = raw.tile([P, 4, NB], BF16, name="s_raw_t", bufs=6, align_bytes=256)
+            nc.sync.dma_start(out=tile_s[:], in_=s_view[c, :, :, n * NB : (n + 1) * NB])
+            s_raw[c, n] = tile_s[:]
+
+        def load_s_wide(c):
+            wide = raw.tile([P, 4, 2 * NB], BF16, name="wide_raw_t", bufs=3, align_bytes=256)
+            nc.sync.dma_start(out=wide[:], in_=s_view[c, :, :, 2 * NB :])
+            for h in range(2):
+                s_raw[c, 2 + h] = wide[:, :, h * NB : (h + 1) * NB]
 
         def bank_tile(b, shape=(P, NB), dtype=F32):
             return psum.tile(list(shape), dtype, name="bank_t", tag=f"bank{b}")
@@ -91,12 +96,13 @@ def tile_rocchio_feedback_rescore_s2_kernel(tc, queries, corpus, relevance, sim,
 
         c_sort = {}
 
-        def sort_c(n, t):
+        def sort_c(n, t, engine="V"):
             if t == 0:
                 c_sort[n] = raw.tile([P, 4, WORDS], F32, name="c_sort_t", bufs=1, align_bytes=256)
-            nc.vector.tensor_copy(
-                out=c_sort[n][:, t, :].rearrange("p (g u w) -> p g u w", g=2, u=2),
-                in_=c_raw[n][:, t, :].bitcast(F32).rearrange("p (g w u) -> p g u w", g=2, u=2),
+            copy_words(
+                engine,
+                c_sort[n][:, t, :].rearrange("p (g u w) -> p g u w", g=2, u=2),
+                c_raw[n][:, t, :].bitcast(F32).rearrange("p (g w u) -> p g u w", g=2, u=2),
             )
 
         q_bank, q_grp = {}, {}
@@ -124,7 +130,7 @@ def tile_rocchio_feedback_rescore_s2_kernel(tc, queries, corpus, relevance, sim,
 
         def turn_c(n, t, b):
             c_bank[n, t] = bank_tile(b)
-            if n < 2:
+            if n == 0:
                 turn(c_raw[n][:, t, :].bitcast(F32), c_bank[n, t])
             else:
                 for s in range(4):
@@ -164,7 +170,7 @@ def tile_rocchio_feedback_rescore_s2_kernel(tc, queries, corpus, relevance, sim,
 
         def copy_r(c, h, engine):
             r_grp[c, h] = stage.tile([P, NB, 4], BF16, name="k_grp_t", bufs=6, align_bytes=256)
-            interleave(engine, r_grp[c, h][:], r_raw[:, c, :, h * NB : (h + 1) * NB])
+            interleave(engine, r_grp[c, h][:], r_raw[c][:, :, h * NB : (h + 1) * NB])
 
         def quant_r(c, h):
             nc.vector.quantize_mx(
@@ -215,8 +221,21 @@ def tile_rocchio_feedback_rescore_s2_kernel(tc, queries, corpus, relevance, sim,
                 stop=(c == J_PASSES - 1),
             )
 
+        def keep_busy(passes):
+            spare = bank_tile(5)
+            for i in range(passes):
+                nc.tensor.matmul_mx(
+                    out=spare[:],
+                    lhsT=q_codes[:, 0, 0, :].bitcast(E4M3X4),
+                    lhsT_scale=q_scales[:, 0, 0, :],
+                    rhs=q_codes[:, 0:2, :, :].rearrange("p m g r -> p (m g r)").bitcast(E4M3X4),
+                    rhs_scale=q_scales[:, 0:2, :, :].rearrange("p m g r -> p (m g r)"),
+                    start=True,
+                    stop=True,
+                )
+
         def finish(n, m, pieces=1):
-            res = stage.tile([P, NB], F32, name="res_t", bufs=8)
+            res = stage.tile([P, NB], F32, name="res_t", bufs=12)
             w = NB // pieces
             for i in range(pieces):
                 cs = slice(i * w, (i + 1) * w)
@@ -231,23 +250,15 @@ def tile_rocchio_feedback_rescore_s2_kernel(tc, queries, corpus, relevance, sim,
                 )
                 nc.sync.dma_start(out=out[m * P : (m + 1) * P, oc], in_=res[:, cs])
 
-        def finish_sg(n, m):
-            part = stage.tile([P, NB], F32, name="part_t", bufs=2)
-            res = stage.tile([P, NB], F32, name="res_t", bufs=8)
-            nc.scalar.activation(
-                out=part[:], in_=acc[n, m][:], func=mybir.ActivationFunctionType.Copy, scale=gain_col[:, m : m + 1]
-            )
-            nc.gpsimd.tensor_tensor(out=res[:], in0=part[:], in1=prior_bc[:, n, :], op=ADD)
-            nc.sync.dma_start(out=out[m * P : (m + 1) * P, n * NB : (n + 1) * NB], in_=res[:])
-
         V, S = "V", "S"
         halves = (range(0, 4), range(4, 8))
 
         nc.vector.memset(rows[:], 0.0)
         load_q(0, 1)
         load_q(1, 2)
+        nc.sync.dma_start(out=rows[0:16, :], in_=prior.rearrange("(a b) -> a b", b=P))
+        nc.sync.dma_start(out=rows[16:24, :], in_=gain.rearrange("(a b) -> a b", b=P))
         load_q(2, 4)
-        nc.sync.dma_start(out=rows[0:8, :], in_=gain.rearrange("(a b) -> a b", b=P))
         load_r(0)
         load_q(4, 6)
         load_q(6, 8)
@@ -256,12 +267,10 @@ def tile_rocchio_feedback_rescore_s2_kernel(tc, queries, corpus, relevance, sim,
         load_s(0, 0)
         load_s(1, 0)
         load_r(2)
-        load_prior(0)
         load_s(2, 0)
         load_c(1)
         for c in range(3):
             load_s(c, 1)
-        load_prior(1)
 
         make_identity(nc, ident[:])
         nc.vector.tensor_copy(out=ident_bf[:], in_=ident[:])
@@ -269,19 +278,28 @@ def tile_rocchio_feedback_rescore_s2_kernel(tc, queries, corpus, relevance, sim,
         for m in (0, 1):
             turn_q(m, m)
             copy_q(m, S)
+        rows_t = bank_tile(7, (P, P), BF16)
+        nc.tensor.transpose(rows_t[:], rows[:], ident_bf[:])
+        nc.vector.tensor_copy(out=cols[:], in_=rows_t[:, 0:24])
+        nc.vector.tensor_copy(out=gain_col[:], in_=rows_t[:, 16:24])
         quant_q(0)
         quant_q(1)
-        copy_r(0, 0, V)
-        copy_r(0, 1, S)
         for m in (2, 3):
             turn_q(m, m)
-            copy_q(m, V)
+            copy_q(m, (S, V)[m % 2])
+        for h in range(2):
+            spread = bank_tile(4 + h, (P, M), BF16)
+            for i in range(8):
+                nc.tensor.transpose(
+                    spread[:, i * P : (i + 1) * P], cols[:, 8 * h + i : 8 * h + i + 1].to_broadcast([P, P]), ident_bf[:]
+                )
+            copy_words((V, S)[h], prior_bc[:, 2 * h : 2 * h + 2, :].rearrange("p n w -> p (n w)"), spread[:])
+        copy_r(0, 0, V)
+        copy_r(0, 1, S)
         quant_r(0, 0)
         for m in range(4, 8):
             turn_q(m, m)
             copy_q(m, S)
-        rows_t = bank_tile(0, (P, P), BF16)
-        nc.tensor.transpose(rows_t[:], rows[:], ident_bf[:])
         quant_q(2)
         quant_q(3)
         quant_r(0, 1)
@@ -293,11 +311,11 @@ def tile_rocchio_feedback_rescore_s2_kernel(tc, queries, corpus, relevance, sim,
             copy_c(0, t, (S, V)[t % 2])
             if t == 2:
                 quant_q(7)
-                nc.vector.tensor_copy(out=gain_col[:], in_=rows_t[:, 0:8])
                 quant_c(0, 0, 0)
         quant_c(0, 0, 1)
         quant_c(0, 1, 0)
         quant_c(0, 1, 1)
+        keep_busy(3)
         for g in range(2):
             for m in range(8):
                 pass_qc(0, m, g, m)
@@ -321,14 +339,19 @@ def tile_rocchio_feedback_rescore_s2_kernel(tc, queries, corpus, relevance, sim,
         quant_r(2, 1)
         load_c(2)
         for c in range(3):
-            load_s(c, 2)
-        load_prior(2)
+            load_s_wide(c)
         for m in range(0, 4):
             pass_rs(0, m, 2)
+        sort_c(1, 0, S)
+        sort_c(1, 1, S)
+        sort_c(1, 2)
+        sort_c(1, 3)
         finish(0, 0)
-        finish_sg(0, 1)
+        finish(0, 1)
         finish(0, 2)
-        finish_sg(0, 3)
+        finish(0, 3)
+        load_c(3)
+        copy_s(0, 1, S)
         for h in range(2):
             for t in (2 * h, 2 * h + 1):
                 turn_c(1, t, t)
@@ -343,16 +366,11 @@ def tile_rocchio_feedback_rescore_s2_kernel(tc, queries, corpus, relevance, sim,
             quant_c(1, g, 1)
         finish(0, 6)
         finish(0, 7)
-        copy_s(0, 1, V + S)
-        copy_s(1, 1, V + S)
         quant_s(0, 1)
+        copy_s(1, 1, V + S)
         copy_s(2, 1, V + S)
         quant_s(1, 1)
 
-        load_c(3)
-        for c in range(3):
-            load_s(c, 3)
-        load_prior(3)
         for n in range(1, N_BLOCKS):
             more = n + 1 < N_BLOCKS
             if n == 1:

@@ -112,7 +112,7 @@ def tile_rocchio_feedback_rescore_s2_kernel(tc, queries, corpus, relevance, sim,
             turn(q_raw[:, m, :].bitcast(F32), q_bank[m])
 
         def copy_q(m, engine):
-            q_grp[m] = stage.tile([P, E_PASSES, P, 4], BF16, name="q_grp_t", align_bytes=256)
+            q_grp[m] = stage.tile([P, E_PASSES, P, 4], BF16, name="q_grp_t", bufs=6, align_bytes=256)
             copy_words(
                 engine,
                 q_grp[m][:].rearrange("p g r j -> p (g r j)").bitcast(F32).rearrange("p (g r u) -> p g r u", g=2, u=2),
@@ -221,6 +221,30 @@ def tile_rocchio_feedback_rescore_s2_kernel(tc, queries, corpus, relevance, sim,
                 stop=(c == J_PASSES - 1),
             )
 
+        def load_vectors():
+            nc.sync.dma_start(out=rows[0:16, :], in_=prior.rearrange("(a b) -> a b", b=P))
+            nc.sync.dma_start(out=rows[16:24, :], in_=gain.rearrange("(a b) -> a b", b=P))
+
+        vec = {}
+
+        def turn_vectors():
+            vec["rows"] = bank_tile(7, (P, P), BF16)
+            nc.tensor.transpose(vec["rows"][:], rows[:], ident_bf[:])
+
+        def copy_vectors():
+            nc.vector.tensor_copy(out=cols[:], in_=vec["rows"][:, 0:24])
+            nc.vector.tensor_copy(out=gain_col[:], in_=vec["rows"][:, 16:24])
+
+        def turn_prior(h):
+            vec[h] = bank_tile(4 + h, (P, M), BF16)
+            for i in range(8):
+                nc.tensor.transpose(
+                    vec[h][:, i * P : (i + 1) * P], cols[:, 8 * h + i : 8 * h + i + 1].to_broadcast([P, P]), ident_bf[:]
+                )
+
+        def copy_prior(h, engine):
+            copy_words(engine, prior_bc[:, 2 * h : 2 * h + 2, :].rearrange("p n w -> p (n w)"), vec[h][:])
+
         def keep_busy(passes):
             spare = bank_tile(5)
             for i in range(passes):
@@ -256,8 +280,7 @@ def tile_rocchio_feedback_rescore_s2_kernel(tc, queries, corpus, relevance, sim,
         nc.vector.memset(rows[:], 0.0)
         load_q(0, 1)
         load_q(1, 2)
-        nc.sync.dma_start(out=rows[0:16, :], in_=prior.rearrange("(a b) -> a b", b=P))
-        nc.sync.dma_start(out=rows[16:24, :], in_=gain.rearrange("(a b) -> a b", b=P))
+        load_vectors()
         load_q(2, 4)
         load_r(0)
         load_q(4, 6)
@@ -278,22 +301,16 @@ def tile_rocchio_feedback_rescore_s2_kernel(tc, queries, corpus, relevance, sim,
         for m in (0, 1):
             turn_q(m, m)
             copy_q(m, S)
-        rows_t = bank_tile(7, (P, P), BF16)
-        nc.tensor.transpose(rows_t[:], rows[:], ident_bf[:])
-        nc.vector.tensor_copy(out=cols[:], in_=rows_t[:, 0:24])
-        nc.vector.tensor_copy(out=gain_col[:], in_=rows_t[:, 16:24])
+        turn_vectors()
+        copy_vectors()
         quant_q(0)
         quant_q(1)
         for m in (2, 3):
             turn_q(m, m)
             copy_q(m, (S, V)[m % 2])
         for h in range(2):
-            spread = bank_tile(4 + h, (P, M), BF16)
-            for i in range(8):
-                nc.tensor.transpose(
-                    spread[:, i * P : (i + 1) * P], cols[:, 8 * h + i : 8 * h + i + 1].to_broadcast([P, P]), ident_bf[:]
-                )
-            copy_words((V, S)[h], prior_bc[:, 2 * h : 2 * h + 2, :].rearrange("p n w -> p (n w)"), spread[:])
+            turn_prior(h)
+            copy_prior(h, (V, S)[h])
         copy_r(0, 0, V)
         copy_r(0, 1, S)
         quant_r(0, 0)

from contextlib import ExitStack

import concourse.mybir as mybir
from concourse.masks import make_identity

F32 = mybir.dt.float32
BF16 = mybir.dt.bfloat16
U32 = mybir.dt.uint32
U8 = mybir.dt.uint8
E4M3X4 = mybir.dt.float8_e4m3fn_x4
E5M2X4 = mybir.dt.float8_e5m2_x4
MULT = mybir.AluOpType.mult
ADD = mybir.AluOpType.add

M, N, E, J = 1024, 2048, 1024, 1536
FLOPS = 2 * M * N * (E + J)

P = 128
K_PASS = 512
E_PASSES = E // K_PASS
J_PASSES = J // K_PASS
NB = 512
M_TILES = M // P
N_BLOCKS = N // NB
WORDS = E // 2


def tile_rocchio_feedback_rescore_s2_kernel(tc, queries, corpus, relevance, sim, gain, prior, out):
    nc = tc.nc
    with ExitStack() as ctx:
        keep = ctx.enter_context(tc.tile_pool(name="keep", bufs=1))
        raw = ctx.enter_context(tc.tile_pool(name="raw", bufs=1))
        stage = ctx.enter_context(tc.tile_pool(name="stage", bufs=3))
        psum = ctx.enter_context(tc.psum_pool(name="psum", bufs=1))
        ctx.enter_context(tc.manual_schedule())

        ident = keep.tile([P, P], F32, name="ident")
        ident_bf = keep.tile([P, P], BF16, name="ident_bf")
        rows = keep.tile([P, P], BF16, name="rows")
        cols = keep.tile([P, 24], BF16, name="cols")
        gain_col = keep.tile([P, M_TILES], F32, name="gain_col")
        prior_bc = keep.tile([P, N_BLOCKS, NB], BF16, name="prior_bc")

        q_codes = keep.tile([P, M_TILES, E_PASSES, P], U32, name="q_codes", align_bytes=256)
        q_scales = keep.tile([P, M_TILES, E_PASSES, P], U8, name="q_scales", align_bytes=256)
        r_codes = keep.tile([P, J_PASSES, M], U32, name="r_codes", align_bytes=256)
        r_scales = keep.tile([P, J_PASSES, M], U8, name="r_scales", align_bytes=256)
        q_raw = raw.tile([P, M_TILES, E], BF16, name="q_raw", align_bytes=256)
        r_raw, c_raw, s_raw, c_codes, c_scales, s_codes, s_scales = {}, {}, {}, {}, {}, {}, {}

        q_view = queries.rearrange("(t p) e -> p t e", p=P)
        c_view = corpus.rearrange("(t p) e -> p t e", p=P)
        r_view = relevance.rearrange("(c p j) m -> c p j m", p=P, j=4)
        s_view = sim.rearrange("(c p j) n -> c p j n", p=P, j=4)

        def load_q(t0, t1):
            nc.sync.dma_start(out=q_raw[:, t0:t1, :], in_=q_view[:, t0:t1, :])

        def load_r(c):
            r_raw[c] = raw.tile([P, 4, M], BF16, name="wide_raw_t", bufs=3, align_bytes=256)
            nc.sync.dma_start(out=r_raw[c][:], in_=r_view[c])

        def load_c(n):
            c_raw[n] = raw.tile([P, 4, E], BF16, name="c_raw_t", bufs=3, align_bytes=256)
            step = 1 if n == 0 else 2
            for t in range(0, 4, step):
                nc.sync.dma_start(out=c_raw[n][:, t : t + step, :], in_=c_view[:, 4 * n + t : 4 * n + t + step, :])

        def load_s(c, n):
            tile_s = raw.tile([P, 4, NB], BF16, name="s_raw_t", bufs=6, align_bytes=256)
            nc.sync.dma_start(out=tile_s[:], in_=s_view[c, :, :, n * NB : (n + 1) * NB])
            s_raw[c, n] = tile_s[:]

        def load_s_wide(c):
            wide = raw.tile([P, 4, 2 * NB], BF16, name="wide_raw_t", bufs=3, align_bytes=256)
            nc.sync.dma_start(out=wide[:], in_=s_view[c, :, :, 2 * NB :])
            for h in range(2):
                s_raw[c, 2 + h] = wide[:, :, h * NB : (h + 1) * NB]

        def bank_tile(b, shape=(P, NB), dtype=F32):
            return psum.tile(list(shape), dtype, name="bank_t", tag=f"bank{b}")

        def copy_words(engine, dst, src):
            if engine == "S":
                nc.scalar.copy(out=dst, in_=src)
            else:
                nc.vector.tensor_copy(out=dst, in_=src)

        def turn(words, bank):
            for g in range(E_PASSES):
                for u in range(2):
                    s = 2 * g + u
                    nc.tensor.transpose(
                        bank[:, s * P : (s + 1) * P], words[:, 256 * g + u : 256 * (g + 1) : 2], ident[:]
                    )

        c_sort = {}

        def sort_c(n, t, engine="V"):
            if t == 0:
                c_sort[n] = raw.tile([P, 4, WORDS], F32, name="c_sort_t", bufs=1, align_bytes=256)
            copy_words(
                engine,
                c_sort[n][:, t, :].rearrange("p (g u w) -> p g u w", g=2, u=2),
                c_raw[n][:, t, :].bitcast(F32).rearrange("p (g w u) -> p g u w", g=2, u=2),
            )

        q_bank, q_grp = {}, {}

        def turn_q(m, b):
            q_bank[m] = bank_tile(b)
            turn(q_raw[:, m, :].bitcast(F32), q_bank[m])

        def copy_q(m, engine):
            q_grp[m] = stage.tile([P, E_PASSES, P, 4], BF16, name="q_grp_t", bufs=6, align_bytes=256)
            copy_words(
                engine,
                q_grp[m][:].rearrange("p g r j -> p (g r j)").bitcast(F32).rearrange("p (g r u) -> p g r u", g=2, u=2),
                q_bank[m][:].rearrange("p (g u r) -> p g r u", g=2, u=2),
            )

        def quant_q(m):
            nc.vector.quantize_mx(
                out=q_codes[:, m, :, :].rearrange("p g r -> p (g r)").bitcast(E4M3X4),
                scales=q_scales[:, m, :, :].rearrange("p g r -> p (g r)"),
                in_=q_grp[m][:].rearrange("p g r j -> p (g r j)"),
            )

        c_bank, c_grp = {}, {}

        def turn_c(n, t, b):
            c_bank[n, t] = bank_tile(b)
            if n == 0:
                turn(c_raw[n][:, t, :].bitcast(F32), c_bank[n, t])
            else:
                for s in range(4):
                    nc.tensor.transpose(
                        c_bank[n, t][:, s * P : (s + 1) * P], c_sort[n][:, t, s * P : (s + 1) * P], ident[:]
                    )

        def copy_c(n, t, engine):
            if t == 0:
                c_grp[n] = stage.tile([P, E_PASSES, NB, 4], BF16, name="c_grp_t", bufs=2, align_bytes=256)
            words = c_grp[n][:].rearrange("p g r j -> p (g r j)").bitcast(F32)
            copy_words(
                engine,
                words.rearrange("p (g r u) -> p g r u", g=2, u=2)[:, :, t * P : (t + 1) * P, :],
                c_bank[n, t][:].rearrange("p (g u r) -> p g r u", g=2, u=2),
            )

        def quant_c(n, g, h):
            if g == 0 and h == 0:
                c_codes[n] = stage.tile([P, E_PASSES, NB], U32, name="c_codes_t", bufs=2, align_bytes=256)
                c_scales[n] = stage.tile([P, E_PASSES, NB], U8, name="c_scales_t", bufs=2, align_bytes=256)
            cs = slice(h * 256, (h + 1) * 256)
            nc.vector.quantize_mx(
                out=c_codes[n][:, g, cs].bitcast(E4M3X4),
                scales=c_scales[n][:, g, cs],
                in_=c_grp[n][:, g, cs, :].rearrange("p r j -> p (r j)"),
            )

        r_grp, s_grp = {}, {}

        def interleave(engine, dst, src):
            copy_words(
                engine,
                dst.rearrange("p (c i) j -> p c j i", i=4),
                src.rearrange("p j (c i) -> p c j i", i=4),
            )

        def copy_r(c, h, engine):
            r_grp[c, h] = stage.tile([P, NB, 4], BF16, name="k_grp_t", bufs=6, align_bytes=256)
            interleave(engine, r_grp[c, h][:], r_raw[c][:, :, h * NB : (h + 1) * NB])

        def quant_r(c, h):
            nc.vector.quantize_mx(
                out=r_codes[:, c, h * NB : (h + 1) * NB].bitcast(E5M2X4),
                scales=r_scales[:, c, h * NB : (h + 1) * NB],
                in_=r_grp[c, h][:].rearrange("p w j -> p (w j)"),
            )

        def copy_s(c, n, engines):
            s_grp[c, n] = stage.tile([P, NB, 4], BF16, name="k_grp_t", bufs=6, align_bytes=256)
            w = NB // len(engines)
            for i, engine in enumerate(engines):
                cs = slice(i * w, (i + 1) * w)
                interleave(engine, s_grp[c, n][:, cs, :], s_raw[c, n][:, :, cs])

        def quant_s(c, n):
            s_codes[c, n] = stage.tile([P, NB], U32, name="s_codes_t", bufs=7, align_bytes=256)
            s_scales[c, n] = stage.tile([P, NB], U8, name="s_scales_t", bufs=7, align_bytes=256)
            nc.vector.quantize_mx(
                out=s_codes[c, n][:].bitcast(E4M3X4),
                scales=s_scales[c, n][:],
                in_=s_grp[c, n][:].rearrange("p w j -> p (w j)"),
            )

        acc = {}

        def pass_qc(n, m, g, b):
            if g == 0:
                acc[n, m] = bank_tile(b)
            nc.tensor.matmul_mx(
                out=acc[n, m][:],
                lhsT=q_codes[:, m, g, :].bitcast(E4M3X4),
                lhsT_scale=q_scales[:, m, g, :],
                rhs=c_codes[n][:, g, :].bitcast(E4M3X4),
                rhs_scale=c_scales[n][:, g, :],
                start=(g == 0),
                stop=False,
            )

        def pass_rs(n, m, c):
            nc.tensor.matmul_mx(
                out=acc[n, m][:],
                lhsT=r_codes[:, c, m * P : (m + 1) * P].bitcast(E5M2X4),
                lhsT_scale=r_scales[:, c, m * P : (m + 1) * P],
                rhs=s_codes[c, n][:].bitcast(E4M3X4),
                rhs_scale=s_scales[c, n][:],
                start=False,
                stop=(c == J_PASSES - 1),
            )

        def load_vectors():
            nc.sync.dma_start(out=rows[0:16, :], in_=prior.rearrange("(a b) -> a b", b=P))
            nc.sync.dma_start(out=rows[16:24, :], in_=gain.rearrange("(a b) -> a b", b=P))

        vec = {}

        def turn_vectors():
            vec["rows"] = bank_tile(7, (P, P), BF16)
            nc.tensor.transpose(vec["rows"][:], rows[:], ident_bf[:])

        def copy_vectors():
            nc.vector.tensor_copy(out=cols[:], in_=vec["rows"][:, 0:24])
            nc.vector.tensor_copy(out=gain_col[:], in_=vec["rows"][:, 16:24])

        def turn_prior(h):
            vec[h] = bank_tile(4 + h, (P, M), BF16)
            for i in range(8):
                nc.tensor.transpose(
                    vec[h][:, i * P : (i + 1) * P], cols[:, 8 * h + i : 8 * h + i + 1].to_broadcast([P, P]), ident_bf[:]
                )

        def copy_prior(h, engine):
            copy_words(engine, prior_bc[:, 2 * h : 2 * h + 2, :].rearrange("p n w -> p (n w)"), vec[h][:])

        def keep_busy(passes):
            spare = bank_tile(5)
            for i in range(passes):
                nc.tensor.matmul_mx(
                    out=spare[:],
                    lhsT=q_codes[:, 0, 0, :].bitcast(E4M3X4),
                    lhsT_scale=q_scales[:, 0, 0, :],
                    rhs=q_codes[:, 0:2, :, :].rearrange("p m g r -> p (m g r)").bitcast(E4M3X4),
                    rhs_scale=q_scales[:, 0:2, :, :].rearrange("p m g r -> p (m g r)"),
                    start=True,
                    stop=True,
                )

        def finish(n, m, pieces=1):
            res = stage.tile([P, NB], F32, name="res_t", bufs=12)
            w = NB // pieces
            for i in range(pieces):
                cs = slice(i * w, (i + 1) * w)
                oc = slice(n * NB + i * w, n * NB + (i + 1) * w)
                nc.vector.scalar_tensor_tensor(
                    out=res[:, cs],
                    in0=acc[n, m][:, cs],
                    scalar=gain_col[:, m : m + 1],
                    in1=prior_bc[:, n, cs],
                    op0=MULT,
                    op1=ADD,
                )
                nc.sync.dma_start(out=out[m * P : (m + 1) * P, oc], in_=res[:, cs])

        V, S = "V", "S"
        halves = (range(0, 4), range(4, 8))

        nc.vector.memset(rows[:], 0.0)
        load_q(0, 1)
        load_q(1, 2)
        load_vectors()
        load_q(2, 4)
        load_r(0)
        load_q(4, 6)
        load_q(6, 8)
        load_c(0)
        load_r(1)
        load_s(0, 0)
        load_s(1, 0)
        load_r(2)
        load_s(2, 0)
        load_c(1)
        for c in range(3):
            load_s(c, 1)

        make_identity(nc, ident[:])
        nc.vector.tensor_copy(out=ident_bf[:], in_=ident[:])

        for m in (0, 1):
            turn_q(m, m)
            copy_q(m, S)
        turn_vectors()
        copy_vectors()
        quant_q(0)
        quant_q(1)
        for m in (2, 3):
            turn_q(m, m)
            copy_q(m, (S, V)[m % 2])
        for h in range(2):
            turn_prior(h)
            copy_prior(h, (V, S)[h])
        copy_r(0, 0, V)
        copy_r(0, 1, S)
        quant_r(0, 0)
        for m in range(4, 8):
            turn_q(m, m)
            copy_q(m, S)
        quant_q(2)
        quant_q(3)
        quant_r(0, 1)
        quant_q(4)
        quant_q(5)
        quant_q(6)
        for t in range(4):
            turn_c(0, t, 1 + t)
            copy_c(0, t, (S, V)[t % 2])
            if t == 2:
                quant_q(7)
                quant_c(0, 0, 0)
        quant_c(0, 0, 1)
        quant_c(0, 1, 0)
        quant_c(0, 1, 1)
        keep_busy(3)
        for g in range(2):
            for m in range(8):
                pass_qc(0, m, g, m)
        copy_r(1, 0, S)
        copy_r(1, 1, V)
        copy_s(0, 0, V)
        quant_r(1, 1)
        quant_s(0, 0)
        quant_r(1, 0)
        copy_s(1, 0, S)
        for m in range(8):
            pass_rs(0, m, 0)
        copy_r(2, 0, V)
        copy_r(2, 1, S)
        quant_s(1, 0)
        copy_s(2, 0, V + S)
        quant_r(2, 0)
        for m in range(8):
            pass_rs(0, m, 1)
        quant_s(2, 0)
        quant_r(2, 1)
        load_c(2)
        for c in range(3):
            load_s_wide(c)
        for m in range(0, 4):
            pass_rs(0, m, 2)
        sort_c(1, 0, S)
        sort_c(1, 1, S)
        sort_c(1, 2)
        sort_c(1, 3)
        finish(0, 0)
        finish(0, 1)
        finish(0, 2)
        finish(0, 3)
        load_c(3)
        copy_s(0, 1, S)
        for h in range(2):
            for t in (2 * h, 2 * h + 1):
                turn_c(1, t, t)
                copy_c(1, t, S)
            for m in (4 + 2 * h, 5 + 2 * h):
                pass_rs(0, m, 2)
        finish(0, 4)
        for g in range(2):
            quant_c(1, g, 0)
        finish(0, 5)
        for g in range(2):
            quant_c(1, g, 1)
        finish(0, 6)
        finish(0, 7)
        quant_s(0, 1)
        copy_s(1, 1, V + S)
        copy_s(2, 1, V + S)
        quant_s(1, 1)

        for n in range(1, N_BLOCKS):
            more = n + 1 < N_BLOCKS
            if n == 1:
                for g in range(2):
                    for m in range(6):
                        pass_qc(n, m, g, m)
                quant_s(2, 1)
                for t in range(4):
                    sort_c(2, t)
                copy_s(0, 2, S)
                for c in range(2):
                    for m in range(4):
                        pass_rs(n, m, c)
                for h in range(2):
                    for t in (2 * h, 2 * h + 1):
                        turn_c(2, t, 6 + t % 2)
                        copy_c(2, t, S)
                    for m in (2 * h, 2 * h + 1):
                        pass_rs(n, m, 2)
                        finish(n, m)
                    for g in range(2):
                        quant_c(2, g, h)
            for m in range(M_TILES):
                if n > 1 or m > 5:
                    for g in range(2):
                        pass_qc(n, m, g, m)
                if n > 1 or m > 3:
                    for c in range(3):
                        pass_rs(n, m, c)
                if more:
                    if m == 0 and n == 2:
                        copy_s(0, n + 1, S)
                    if m == 2:
                        copy_s(1, n + 1, S)
                    if m == 3:
                        quant_s(0, n + 1)
                    if m < 4 and n == 2:
                        sort_c(n + 1, m)
                    if m == 3 and n == 2:
                        for t in range(4):
                            turn_c(n + 1, t, t if t < 3 else 7)
                            copy_c(n + 1, t, S)
                if n > 1 or m > 3:
                    finish(n, m, 2 if m == 7 and not more else 1)
                if more:
                    if m == 4:
                        copy_s(2, n + 1, V + S)
                        if n == 2:
                            for h in range(2):
                                for g in range(2):
                                    quant_c(n + 1, g, h)
                    if m == 5:
                        quant_s(1, n + 1)
                        quant_s(2, n + 1)
